import numpy as np
import ml_dtypes


def mxq(x, axis, fmt="e4m3"):
    dtype, down = {"e4m3": (ml_dtypes.float8_e4m3fn, 7), "e5m2": (ml_dtypes.float8_e5m2, 14)}[fmt]
    v = np.moveaxis(np.asarray(x, np.float32).astype(ml_dtypes.bfloat16).astype(np.float64), axis, -1)
    blocks = v.reshape(v.shape[:-1] + (-1, 32))
    amax = np.abs(blocks).max(-1, keepdims=True)
    byte = np.maximum(np.where(amax > 0, np.frexp(amax)[1] - 1 + 127, 0) - down, 1)
    scale = np.exp2(byte - 127.0)
    codes = (blocks / scale).astype(np.float32).astype(dtype).astype(np.float64)
    return np.moveaxis((codes * scale).reshape(v.shape), -1, axis)


WIDE = False


def mx_kscale(k):
    if not WIDE:
        return np.ones(k)
    levels = np.array([10, -10, 5, -5, 0])
    if k % 512:
        return np.exp2(np.random.permutation(np.resize(levels, k // 32))).repeat(32)
    a = np.empty((k // 512, 16))
    for p in range(k // 512):
        a[p, :8] = np.random.permutation(np.resize(levels, 8))
        for g in range(8):
            far = levels[np.abs(levels - a[p, g]) >= 10]
            a[p, g + 8] = far[np.random.randint(len(far))]
    return np.exp2(a.ravel()).repeat(32)


def f64(x):
    return np.asarray(x).astype(np.float64)


def striped(idx):
    return np.tile(np.asarray(idx).reshape(-1, 16).T, (8, 1)).astype(np.uint16)


def unstriped(offs):
    return offs[:16].T.reshape(-1).astype(np.int64)


E2M1 = np.array([0.0, 0.5, 1.0, 1.5, 2.0, 3.0, 4.0, 6.0, -0.0, -0.5, -1.0, -1.5, -2.0, -3.0, -4.0, -6.0])


def pack_weight(w, fmt):
    k, n = w.shape
    w = f64(np.asarray(w, np.float32).astype(ml_dtypes.bfloat16)).reshape(k // 32, 32, n)
    amax = np.abs(w).max(1)
    if fmt == "e4m3":
        byte = np.frexp(amax)[1] - 1 + 127 - 7
    else:
        mant, ex = np.frexp(amax / 6.0)
        byte = np.where(mant > 0.5, ex, ex - 1) + 127
    byte = np.clip(np.where(amax > 0, byte, 1), 1, 254)
    scaled = (w * np.exp2(127.0 - byte)[:, None, :]).reshape(k, n).astype(np.float32)
    by_word = np.ascontiguousarray(scaled.reshape(k // 512, 128, 4, n).transpose(0, 1, 3, 2))
    if fmt == "e4m3":
        words = by_word.astype(ml_dtypes.float8_e4m3fn).view(np.uint8)
    else:
        c = by_word.astype(ml_dtypes.float4_e2m1fn).view(np.uint8) & 0xF
        words = (c[..., 0::2] | (c[..., 1::2] << 4)).reshape(k // 512, 128, 2 * n)
    return np.ascontiguousarray(words), np.ascontiguousarray(byte.astype(np.uint8).reshape(k // 512, 16, n))


def unpack_weight(words, scales, fmt):
    g, _, n = scales.shape
    words = np.ascontiguousarray(words).reshape(g, 128, n, -1)
    if fmt == "e4m3":
        vals = words.view(ml_dtypes.float8_e4m3fn).astype(np.float64)
    else:
        nib = np.empty((g, 128, n, 4), np.uint8)
        nib[..., 0::2] = words & 0xF
        nib[..., 1::2] = words >> 4
        vals = E2M1[nib]
    vals = vals * np.repeat(np.exp2(scales.astype(np.float64) - 127.0), 8, axis=1)[..., None]
    return vals.transpose(0, 1, 3, 2).reshape(g * 512, n)


D, T, I, C, E = 512, 2048, 512, 512, 512


def setup_inputs():
    n = np.random.standard_normal
    idx = np.random.permutation(T)[:I]
    fd = mx_kscale(D)
    fc = mx_kscale(C)
    keysp = pack_weight(n((D, T)) / fd[:, None], "e2m1")
    return {
        "keys_words": keysp[0],
        "keys_scales": keysp[1],
        "kcopy": (n((E, T))).astype(np.float32),
        "wd": (n((D, C)) * 1 / np.sqrt(D) * fd[:, None] * fc).astype(np.float32),
        "wu": (n((C, E)) * 0.7 / np.sqrt(C) / fc[:, None]).astype(np.float32),
        "offs": striped(idx),
    }


def reference(keys_words, keys_scales, kcopy, wd, wu, offs):
    idx = unstriped(offs)
    keysu = unpack_weight(keys_words, keys_scales, "e2m1")
    wdq = mxq(f64(wd), 0, "e4m3")
    keysidxg = keysu[:, idx]
    z = wdq.T @ keysidxg
    wuq = mxq(f64(wu), 0, "e4m3")
    zq = mxq(z, 0, "e4m3")
    v = wuq.T @ zq
    y = f64(kcopy)[:, idx] + v
    return y

@@ -1,0 +1,121 @@
+from contextlib import ExitStack
+
+import concourse.mybir as mybir
+
+D, T, I, C, E = 512, 2048, 512, 512, 512
+FLOPS = 2 * D * C * I + 2 * C * E * I
+
+F32 = mybir.dt.float32
+BF16 = mybir.dt.bfloat16
+I32 = mybir.dt.int32
+U32 = mybir.dt.uint32
+U16 = mybir.dt.uint16
+U8 = mybir.dt.uint8
+FP8X4 = mybir.dt.float8_e4m3fn_x4
+FP4X4 = mybir.dt.float4_e2m1fn_x4
+ADD = mybir.AluOpType.add
+
+P = 128
+PACK = 4
+HALF = 256
+
+
+def tile_attend_latenterror_kernel(tc, keys_words, keys_scales, kcopy, wd, wu, offs, out):
+    nc = tc.nc
+    with ExitStack() as ctx:
+        sb = ctx.enter_context(tc.tile_pool(name="sb", bufs=1))
+        ps = ctx.enter_context(tc.psum_pool(name="ps", bufs=1))
+
+        offsets = sb.tile([P, I // 16], U16, name="offsets")
+        words = sb.tile([P, T], U16, name="words", align_bytes=64)
+        bytes_ = sb.tile([P, T], U8, name="scale_bytes", align_bytes=64)
+        wd_raw = sb.tile([P, PACK, C], F32, name="wd_raw")
+        wu_raw = sb.tile([P, PACK, E], F32, name="wu_raw")
+        kc = [sb.tile([P, T], F32, name="kc%d" % b, align_bytes=64) for b in range(4)]
+
+        nc.vector.memset(bytes_[:].bitcast(I32), 0)
+        nc.sync.dma_start(offsets[:], offs)
+        nc.sync.dma_start(words[:].bitcast(I32), keys_words[0].bitcast(I32))
+        for r in range(4):
+            nc.sync.dma_start(bytes_[r:P:32, :].bitcast(I32), keys_scales[0, r:16:4, :].bitcast(I32))
+        nc.sync.dma_start(wd_raw[:], wd.rearrange("(p j) c -> p j c", j=PACK))
+        nc.sync.dma_start(wu_raw[:], wu.rearrange("(p j) e -> p j e", j=PACK))
+        for b in range(4):
+            nc.sync.dma_start(kc[b][:], kcopy[b * P:(b + 1) * P, :])
+
+        key_codes = sb.tile([P, I], U16, name="key_codes", align_bytes=64)
+        key_scales = sb.tile([P, I], U8, name="key_scales", align_bytes=64)
+        nc.vector.tensor_copy(key_codes[:], words[:].indirect(offsets[:]))
+        nc.vector.tensor_copy(key_scales[:], bytes_[:].indirect(offsets[:]))
+
+        copies = (nc.vector.tensor_copy, nc.scalar.copy)
+
+        def quantize(name, src, width):
+            codes = sb.tile([P, width], U32, name=name + "_codes", align_bytes=64)
+            scales = sb.tile([P, width], U8, name=name + "_scales", align_bytes=64)
+            nc.vector.quantize_mx(out=codes[:].bitcast(FP8X4), scales=scales[:], in_=src)
+            return codes, scales
+
+        wd_dealt = wd_raw[:].rearrange("p j (m t) -> p m j t", t=PACK)
+        wd_bf = []
+        for h in range(2):
+            w = sb.tile([P, 2, P, PACK], BF16, name="wd_bf%d" % h, align_bytes=64)
+            copies[h](w[:].rearrange("p t m j -> p m j t"), wd_dealt[:, :, :, 2 * h:2 * h + 2])
+            wd_bf.append(w)
+        wd_q = [quantize("wd%d" % h, wd_bf[h][:].rearrange("p t m j -> p (t m j)"), HALF) for h in range(2)]
+
+        z_ps = [ps.tile([P, PACK, P], F32, name="z_ps%d" % b) for b in range(4)]
+        for t in range(PACK):
+            codes, scales = wd_q[t // 2]
+            cols = slice((t % 2) * P, (t % 2 + 1) * P)
+            for b in range(4):
+                slots = slice(b * P, (b + 1) * P)
+                nc.tensor.matmul_mx(
+                    out=z_ps[b][:, t, :],
+                    lhsT=codes[:, cols].bitcast(FP8X4), lhsT_scale=scales[:, cols],
+                    rhs=key_codes[:, slots].bitcast(FP4X4), rhs_scale=key_scales[:, slots],
+                    start=True, stop=True)
+
+        wu_bf = []
+        for h in range(2):
+            w = sb.tile([P, HALF, PACK], BF16, name="wu_bf%d" % h, align_bytes=64)
+            copies[h](w[:].rearrange("p (c i) j -> p c j i", i=4),
+                      wu_raw[:, :, h * HALF:(h + 1) * HALF].rearrange("p j (c i) -> p c j i", i=4))
+            wu_bf.append(w)
+        wu_q = [quantize("wu%d" % h, wu_bf[h][:].rearrange("p e j -> p (e j)"), HALF) for h in range(2)]
+
+        z_q = []
+        for h in range(2):
+            zb = sb.tile([P, HALF, PACK], BF16, name="z_bf%d" % h, align_bytes=64)
+            for u in range(2):
+                copies[1 - u](zb[:, u * P:(u + 1) * P, :], z_ps[2 * h + u][:].rearrange("p t i -> p i t"))
+            z_q.append(zb)
+        z_q = [quantize("z%d" % h, z_q[h][:].rearrange("p i t -> p (i t)"), HALF) for h in range(2)]
+
+        v_ps = [ps.tile([P, I], F32, name="v_ps%d" % b) for b in range(4)]
+        for b in range(4):
+            codes, scales = wu_q[b // 2]
+            cols = slice((b % 2) * P, (b % 2 + 1) * P)
+            for h in range(2):
+                nc.tensor.matmul_mx(
+                    out=v_ps[b][:, h * HALF:(h + 1) * HALF],
+                    lhsT=codes[:, cols].bitcast(FP8X4), lhsT_scale=scales[:, cols],
+                    rhs=z_q[h][0][:].bitcast(FP8X4), rhs_scale=z_q[h][1][:],
+                    start=True, stop=True)
+
+        picked = sb.tile([P, I], F32, name="picked")
+        nc.vector.tensor_copy(picked[:], kc[0][:].indirect(offsets[:]))
+        y0 = sb.tile([P, I], F32, name="y0")
+        nc.vector.tensor_tensor(y0[:], v_ps[0][:], picked[:], ADD)
+        nc.sync.dma_start(out[0:P, :], y0[:])
+        for b in range(1, 4):
+            v = sb.tile([P, I], F32, name="v%d" % b)
+            nc.scalar.copy(v[:], v_ps[b][:])
+            pieces = 2 if b == 3 else 1
+            width = I // pieces
+            for s in range(pieces):
+                y = sb.tile([P, width], F32, name="y%d_%d" % (b, s))
+                cols = slice(s * width, (s + 1) * width)
+                lst = offsets[:, s * width // 16:(s + 1) * width // 16]
+                nc.vector.tensor_tensor(y[:], kc[b][:].indirect(lst), v[:, cols], ADD)
+                nc.sync.dma_start(out[b * P:(b + 1) * P, cols], y[:])

@@ -59,54 +59,64 @@ def tile_attend_latenterror_kernel(tc, keys_words, keys_scales, kcopy, wd, wu, o
         wd_dealt = wd_raw[:].rearrange("p j (m t) -> p m j t", t=PACK)
         wd_bf = []
         for h in range(2):
-            w = sb.tile([P, 2, P, PACK], BF16, name="wd_bf%d" % h, align_bytes=64)
+            w = sb.tile([P, 2, P, PACK], BF16, name="wd_bf%d" % h, tag="w_bf%d" % h, align_bytes=64)
             copies[h](w[:].rearrange("p t m j -> p m j t"), wd_dealt[:, :, :, 2 * h:2 * h + 2])
             wd_bf.append(w)
         wd_q = [quantize("wd%d" % h, wd_bf[h][:].rearrange("p t m j -> p (t m j)"), HALF) for h in range(2)]
 
         z_ps = [ps.tile([P, PACK, P], F32, name="z_ps%d" % b) for b in range(4)]
-        for t in range(PACK):
-            codes, scales = wd_q[t // 2]
-            cols = slice((t % 2) * P, (t % 2 + 1) * P)
-            for b in range(4):
-                slots = slice(b * P, (b + 1) * P)
+        for b in range(4):
+            slots = slice(b * P, (b + 1) * P)
+            for t in range(PACK):
+                codes, scales = wd_q[t // 2]
+                cols = slice((t % 2) * P, (t % 2 + 1) * P)
                 nc.tensor.matmul_mx(
                     out=z_ps[b][:, t, :],
                     lhsT=codes[:, cols].bitcast(FP8X4), lhsT_scale=scales[:, cols],
                     rhs=key_codes[:, slots].bitcast(FP4X4), rhs_scale=key_scales[:, slots],
                     start=True, stop=True)
 
-        wu_bf = []
-        for h in range(2):
-            w = sb.tile([P, HALF, PACK], BF16, name="wu_bf%d" % h, align_bytes=64)
-            copies[h](w[:].rearrange("p (c i) j -> p c j i", i=4),
-                      wu_raw[:, :, h * HALF:(h + 1) * HALF].rearrange("p j (c i) -> p c j i", i=4))
-            wu_bf.append(w)
-        wu_q = [quantize("wu%d" % h, wu_bf[h][:].rearrange("p e j -> p (e j)"), HALF) for h in range(2)]
+        wu_cast = sb.tile([P, E, PACK], BF16, name="wu_cast", tag="w_bf1", align_bytes=64)
 
+        def cast_wu(h):
+            w = wu_cast[:, h * HALF:(h + 1) * HALF, :]
+            nc.vector.tensor_copy(w.rearrange("p (c i) j -> p c j i", i=4),
+                                  wu_raw[:, :, h * HALF:(h + 1) * HALF].rearrange("p j (c i) -> p c j i", i=4))
+            return w.rearrange("p e j -> p (e j)")
+
+        def cast_z(h):
+            zb = sb.tile([P, HALF, PACK], BF16, name="z_bf%d" % h, tag="z_bf%d" % h, align_bytes=64)
+            for u in range(2):
+                nc.scalar.copy(zb[:, u * P:(u + 1) * P, :], z_ps[2 * h + u][:].rearrange("p t i -> p i t"))
+            return zb[:].rearrange("p i t -> p (i t)")
+
+        wu_bf = [cast_wu(h) for h in range(2)]
+        z_bf = [cast_z(h) for h in range(2)]
+        wu_q = []
         z_q = []
         for h in range(2):
-            zb = sb.tile([P, HALF, PACK], BF16, name="z_bf%d" % h, align_bytes=64)
-            for u in range(2):
-                copies[1 - u](zb[:, u * P:(u + 1) * P, :], z_ps[2 * h + u][:].rearrange("p t i -> p i t"))
-            z_q.append(zb)
-        z_q = [quantize("z%d" % h, z_q[h][:].rearrange("p i t -> p (i t)"), HALF) for h in range(2)]
+            wu_q.append(quantize("wu%d" % h, wu_bf[h], HALF))
+            z_q.append(quantize("z%d" % h, z_bf[h], HALF))
 
         v_ps = [ps.tile([P, I], F32, name="v_ps%d" % b) for b in range(4)]
-        for b in range(4):
+        for b, h in ((0, 0), (1, 0), (0, 1), (1, 1), (2, 0), (2, 1), (3, 0), (3, 1)):
             codes, scales = wu_q[b // 2]
             cols = slice((b % 2) * P, (b % 2 + 1) * P)
-            for h in range(2):
-                nc.tensor.matmul_mx(
-                    out=v_ps[b][:, h * HALF:(h + 1) * HALF],
-                    lhsT=codes[:, cols].bitcast(FP8X4), lhsT_scale=scales[:, cols],
-                    rhs=z_q[h][0][:].bitcast(FP8X4), rhs_scale=z_q[h][1][:],
-                    start=True, stop=True)
+            nc.tensor.matmul_mx(
+                out=v_ps[b][:, h * HALF:(h + 1) * HALF],
+                lhsT=codes[:, cols].bitcast(FP8X4), lhsT_scale=scales[:, cols],
+                rhs=z_q[h][0][:].bitcast(FP8X4), rhs_scale=z_q[h][1][:],
+                start=True, stop=True)
 
-        picked = sb.tile([P, I], F32, name="picked")
-        nc.vector.tensor_copy(picked[:], kc[0][:].indirect(offsets[:]))
         y0 = sb.tile([P, I], F32, name="y0")
-        nc.vector.tensor_tensor(y0[:], v_ps[0][:], picked[:], ADD)
+        picked = []
+        for h in range(2):
+            g = sb.tile([P, HALF], F32, name="picked%d" % h, tag="z_bf%d" % h, align_bytes=64)
+            nc.vector.tensor_copy(g[:], kc[0][:].indirect(offsets[:, 16 * h:16 * (h + 1)]))
+            picked.append(g)
+        for h in range(2):
+            cols = slice(h * HALF, (h + 1) * HALF)
+            nc.vector.tensor_tensor(y0[:, cols], v_ps[0][:, cols], picked[h][:], ADD)
         nc.sync.dma_start(out[0:P, :], y0[:])
         for b in range(1, 4):
             v = sb.tile([P, I], F32, name="v%d" % b)

from contextlib import ExitStack

import concourse.mybir as mybir

D, T, I, C, E = 512, 2048, 512, 512, 512
FLOPS = 2 * D * C * I + 2 * C * E * I

F32 = mybir.dt.float32
BF16 = mybir.dt.bfloat16
I32 = mybir.dt.int32
U32 = mybir.dt.uint32
U16 = mybir.dt.uint16
U8 = mybir.dt.uint8
FP8X4 = mybir.dt.float8_e4m3fn_x4
FP4X4 = mybir.dt.float4_e2m1fn_x4
ADD = mybir.AluOpType.add

P = 128
PACK = 4
HALF = 256


def tile_attend_latenterror_kernel(tc, keys_words, keys_scales, kcopy, wd, wu, offs, out):
    nc = tc.nc
    with ExitStack() as ctx:
        sb = ctx.enter_context(tc.tile_pool(name="sb", bufs=1))
        ps = ctx.enter_context(tc.psum_pool(name="ps", bufs=1))

        offsets = sb.tile([P, I // 16], U16, name="offsets")
        words = sb.tile([P, T], U16, name="words", align_bytes=64)
        bytes_ = sb.tile([P, T], U8, name="scale_bytes", align_bytes=64)
        wd_raw = sb.tile([P, PACK, C], F32, name="wd_raw")
        wu_raw = sb.tile([P, PACK, E], F32, name="wu_raw")
        kc = [sb.tile([P, T], F32, name="kc%d" % b, align_bytes=64) for b in range(4)]

        nc.vector.memset(bytes_[:].bitcast(I32), 0)
        nc.sync.dma_start(offsets[:], offs)
        nc.sync.dma_start(words[:].bitcast(I32), keys_words[0].bitcast(I32))
        for r in range(4):
            nc.sync.dma_start(bytes_[r:P:32, :].bitcast(I32), keys_scales[0, r:16:4, :].bitcast(I32))
        nc.sync.dma_start(wd_raw[:], wd.rearrange("(p j) c -> p j c", j=PACK))
        nc.sync.dma_start(wu_raw[:], wu.rearrange("(p j) e -> p j e", j=PACK))
        for b in range(4):
            nc.sync.dma_start(kc[b][:], kcopy[b * P:(b + 1) * P, :])

        key_codes = sb.tile([P, I], U16, name="key_codes", align_bytes=64)
        key_scales = sb.tile([P, I], U8, name="key_scales", align_bytes=64)
        nc.vector.tensor_copy(key_codes[:], words[:].indirect(offsets[:]))
        nc.vector.tensor_copy(key_scales[:], bytes_[:].indirect(offsets[:]))

        copies = (nc.vector.tensor_copy, nc.scalar.copy)

        def quantize(name, src, width):
            codes = sb.tile([P, width], U32, name=name + "_codes", align_bytes=64)
            scales = sb.tile([P, width], U8, name=name + "_scales", align_bytes=64)
            nc.vector.quantize_mx(out=codes[:].bitcast(FP8X4), scales=scales[:], in_=src)
            return codes, scales

        wd_dealt = wd_raw[:].rearrange("p j (m t) -> p m j t", t=PACK)
        wd_bf = []
        for h in range(2):
            w = sb.tile([P, 2, P, PACK], BF16, name="wd_bf%d" % h, tag="w_bf%d" % h, align_bytes=64)
            copies[h](w[:].rearrange("p t m j -> p m j t"), wd_dealt[:, :, :, 2 * h:2 * h + 2])
            wd_bf.append(w)
        wd_q = [quantize("wd%d" % h, wd_bf[h][:].rearrange("p t m j -> p (t m j)"), HALF) for h in range(2)]

        z_ps = [ps.tile([P, PACK, P], F32, name="z_ps%d" % b) for b in range(4)]
        for b in range(4):
            slots = slice(b * P, (b + 1) * P)
            for t in range(PACK):
                codes, scales = wd_q[t // 2]
                cols = slice((t % 2) * P, (t % 2 + 1) * P)
                nc.tensor.matmul_mx(
                    out=z_ps[b][:, t, :],
                    lhsT=codes[:, cols].bitcast(FP8X4), lhsT_scale=scales[:, cols],
                    rhs=key_codes[:, slots].bitcast(FP4X4), rhs_scale=key_scales[:, slots],
                    start=True, stop=True)

        wu_cast = sb.tile([P, E, PACK], BF16, name="wu_cast", tag="w_bf1", align_bytes=64)

        def cast_wu(h):
            w = wu_cast[:, h * HALF:(h + 1) * HALF, :]
            nc.vector.tensor_copy(w.rearrange("p (c i) j -> p c j i", i=4),
                                  wu_raw[:, :, h * HALF:(h + 1) * HALF].rearrange("p j (c i) -> p c j i", i=4))
            return w.rearrange("p e j -> p (e j)")

        def cast_z(h):
            zb = sb.tile([P, HALF, PACK], BF16, name="z_bf%d" % h, tag="z_bf%d" % h, align_bytes=64)
            for u in range(2):
                nc.scalar.copy(zb[:, u * P:(u + 1) * P, :], z_ps[2 * h + u][:].rearrange("p t i -> p i t"))
            return zb[:].rearrange("p i t -> p (i t)")

        wu_bf = [cast_wu(h) for h in range(2)]
        z_bf = [cast_z(h) for h in range(2)]
        wu_q = []
        z_q = []
        for h in range(2):
            wu_q.append(quantize("wu%d" % h, wu_bf[h], HALF))
            z_q.append(quantize("z%d" % h, z_bf[h], HALF))

        v_ps = [ps.tile([P, I], F32, name="v_ps%d" % b) for b in range(4)]
        for b, h in ((0, 0), (1, 0), (0, 1), (1, 1), (2, 0), (2, 1), (3, 0), (3, 1)):
            codes, scales = wu_q[b // 2]
            cols = slice((b % 2) * P, (b % 2 + 1) * P)
            nc.tensor.matmul_mx(
                out=v_ps[b][:, h * HALF:(h + 1) * HALF],
                lhsT=codes[:, cols].bitcast(FP8X4), lhsT_scale=scales[:, cols],
                rhs=z_q[h][0][:].bitcast(FP8X4), rhs_scale=z_q[h][1][:],
                start=True, stop=True)

        y0 = sb.tile([P, I], F32, name="y0")
        picked = []
        for h in range(2):
            g = sb.tile([P, HALF], F32, name="picked%d" % h, tag="z_bf%d" % h, align_bytes=64)
            nc.vector.tensor_copy(g[:], kc[0][:].indirect(offsets[:, 16 * h:16 * (h + 1)]))
            picked.append(g)
        for h in range(2):
            cols = slice(h * HALF, (h + 1) * HALF)
            nc.vector.tensor_tensor(y0[:, cols], v_ps[0][:, cols], picked[h][:], ADD)
        nc.sync.dma_start(out[0:P, :], y0[:])
        for b in range(1, 4):
            v = sb.tile([P, I], F32, name="v%d" % b)
            nc.scalar.copy(v[:], v_ps[b][:])
            pieces = 2 if b == 3 else 1
            width = I // pieces
            for s in range(pieces):
                y = sb.tile([P, width], F32, name="y%d_%d" % (b, s))
                cols = slice(s * width, (s + 1) * width)
                lst = offsets[:, s * width // 16:(s + 1) * width // 16]
                nc.vector.tensor_tensor(y[:], kc[b][:].indirect(lst), v[:, cols], ADD)
                nc.sync.dma_start(out[b * P:(b + 1) * P, cols], y[:])
